import numpy as np
import ml_dtypes


def mxq(x, axis, fmt="e4m3"):
    dtype, down = {"e4m3": (ml_dtypes.float8_e4m3fn, 7), "e5m2": (ml_dtypes.float8_e5m2, 14)}[fmt]
    v = np.moveaxis(np.asarray(x, np.float32).astype(ml_dtypes.bfloat16).astype(np.float64), axis, -1)
    blocks = v.reshape(v.shape[:-1] + (-1, 32))
    amax = np.abs(blocks).max(-1, keepdims=True)
    byte = np.maximum(np.where(amax > 0, np.frexp(amax)[1] - 1 + 127, 0) - down, 1)
    scale = np.exp2(byte - 127.0)
    codes = (blocks / scale).astype(np.float32).astype(dtype).astype(np.float64)
    return np.moveaxis((codes * scale).reshape(v.shape), -1, axis)


WIDE = False


def mx_kscale(k):
    if not WIDE:
        return np.ones(k)
    levels = np.array([10, -10, 5, -5, 0])
    if k % 512:
        return np.exp2(np.random.permutation(np.resize(levels, k // 32))).repeat(32)
    a = np.empty((k // 512, 16))
    for p in range(k // 512):
        a[p, :8] = np.random.permutation(np.resize(levels, 8))
        for g in range(8):
            far = levels[np.abs(levels - a[p, g]) >= 10]
            a[p, g + 8] = far[np.random.randint(len(far))]
    return np.exp2(a.ravel()).repeat(32)


def f64(x):
    return np.asarray(x).astype(np.float64)


def striped(idx):
    return np.tile(idx.reshape(-1, 16).T, (8, 1)).astype(np.uint16)


def unstriped(offs):
    return offs[:16].T.reshape(-1).astype(np.int64)


def pack_weight(w):
    k, n = w.shape
    w = f64(np.asarray(w, np.float32).astype(ml_dtypes.bfloat16)).reshape(k // 32, 32, n)
    amax = np.abs(w).max(1)
    byte = np.clip(np.where(amax > 0, np.frexp(amax)[1] - 1 + 127 - 7, 1), 1, 254)
    scaled = (w * np.exp2(127.0 - byte)[:, None, :]).reshape(k, n).astype(np.float32)
    words = np.ascontiguousarray(scaled.reshape(k // 512, 128, 4, n).transpose(0, 1, 3, 2)).astype(ml_dtypes.float8_e4m3fn).view(np.uint8)
    return words, np.ascontiguousarray(byte.astype(np.uint8).reshape(k // 512, 16, n))


def unpack_weight(words, scales):
    g, p, n, _ = words.shape
    vals = np.ascontiguousarray(words).view(ml_dtypes.float8_e4m3fn).astype(np.float64) * np.repeat(np.exp2(scales.astype(np.float64) - 127.0), 8, axis=1)[..., None]
    return vals.transpose(0, 1, 3, 2).reshape(g * 512, n)


def sigmoid(v):
    return 1.0 / (1.0 + np.exp(-np.maximum(v, -700.0)))


K, T, S, N, H, U = 512, 2048, 256, 512, 512, 1024


def setup_inputs():
    n = np.random.standard_normal
    s = mx_kscale(K)[:, None]
    u = mx_kscale(H)
    packed_xT = pack_weight(n((K, T)) * s)
    return {
        "x_words": packed_xT[0],
        "x_scales": packed_xT[1],
        "w1": (n((K, H)) / np.sqrt(K) / s).astype(np.float32),
        "mem": n((H, U)).astype(np.float32),
        "sl": np.random.uniform(1.0, 2.0, (H, 1)).astype(np.float32),
        "th": (0.5 * n((H, 1))).astype(np.float32),
        "gn": (np.random.uniform(0.5, 1.5, (H, 1)) * u[:, None]).astype(np.float32),
        "w2": (n((H, N)) / np.sqrt(H) / u[:, None]).astype(np.float32),
        "sl2": np.random.uniform(1.0, 2.0, (N, 1)).astype(np.float32),
        "th2": (0.5 * n((N, 1))).astype(np.float32),
        "offs": striped(np.random.permutation(T)[:S]),
        "n1": striped(np.random.permutation(U)[:S]),
        "n2": striped(np.random.permutation(S)),
        "n3": striped(np.random.permutation(U)),
        "n4": striped(np.random.permutation(U)),
        "n5": striped(np.random.permutation(U)),
    }


def reference(x_words, x_scales, w1, mem, sl, th, gn, w2, sl2, th2, offs, n1, n2, n3, n4, n5):
    old = f64(mem)[:, unstriped(n1)]
    xq = unpack_weight(x_words, x_scales)[:, unstriped(offs)]
    y = mxq(f64(w1), 0, "e4m3").T @ xq
    sg = sigmoid(f64(sl) * (y[:, unstriped(n2)] - f64(th)))
    nw = old + sg * (y - old)
    pg = f64(mem).copy()
    pg[:, unstriped(n1)] = nw
    z = f64(gn) * pg
    h = mxq(f64(w2), 0, "e4m3").T @ mxq(z, 0, "e4m3")
    own = sigmoid(f64(sl2) * (h - f64(th2)))
    sg2 = sigmoid(f64(sl2) * (h[:, unstriped(n3)] - f64(th2)))
    return h[:, unstriped(n4)] * own + h[:, unstriped(n5)] * sg2

@@ -1,0 +1,276 @@
+from contextlib import ExitStack
+
+import concourse.mybir as mybir
+
+K, T, S, N, H, U = 512, 2048, 256, 512, 512, 1024
+FLOPS = 2 * K * H * S + 2 * H * N * U
+
+F32 = mybir.dt.float32
+BF16 = mybir.dt.bfloat16
+I32 = mybir.dt.int32
+U32 = mybir.dt.uint32
+U16 = mybir.dt.uint16
+U8 = mybir.dt.uint8
+FP8X4 = mybir.dt.float8_e4m3fn_x4
+ALU = mybir.AluOpType
+COPY = mybir.ActivationFunctionType.Copy
+SIGMOID = mybir.ActivationFunctionType.Sigmoid
+
+P = 128
+PACK = 4
+HALF = 512
+LIST_COLS = 16
+
+
+def tile_picked_layepgemx_none_p_kernel(
+    tc, x_words, x_scales, w1, mem, sl, th, gn, w2, sl2, th2, offs, n1, n2, n3, n4, n5, out
+):
+    nc = tc.nc
+    with ExitStack() as ctx:
+        lists = ctx.enter_context(tc.tile_pool(name="lists", bufs=1))
+        keep = ctx.enter_context(tc.tile_pool(name="keep", bufs=1))
+        ring = ctx.enter_context(tc.tile_pool(name="ring", bufs=3))
+        psum = ctx.enter_context(tc.psum_pool(name="psum", bufs=1))
+
+        def load_list(src, name):
+            dst = lists.tile(list(src.shape), U16, name=name)
+            nc.sync.dma_start(dst[:], src)
+            return dst
+
+        def load_dealt(src, name):
+            dst = keep.tile([P, PACK], F32, name=name)
+            nc.sync.dma_start(dst[:], src.rearrange("(p t) o -> p (t o)", t=PACK))
+            return dst
+
+        def load_plain(src, name):
+            dst = keep.tile([P, PACK], F32, name=name)
+            with nc.allow_non_contiguous_dma(reason="one value a partition"):
+                nc.sync.dma_start(dst[:], src.rearrange("(t p) o -> p (t o)", t=PACK))
+            return dst
+
+        xs = keep.tile([P, T], U8, name="xs", align_bytes=64)
+        nc.vector.memset(xs[:].bitcast(I32), 0)
+        w1_raw = keep.tile([P, PACK, H], F32, name="w1_raw")
+        nc.sync.dma_start(w1_raw[:], w1.rearrange("(p j) c -> p j c", j=PACK))
+        offs_t = load_list(offs, "offs_t")
+        n1_t = load_list(n1, "n1_t")
+        for q in range(4):
+            nc.sync.dma_start(xs[32 * q : 32 * q + 4, :].bitcast(I32), x_scales[0, 4 * q : 4 * q + 4, :].bitcast(I32))
+        xw = keep.tile([P, T], I32, name="xw", align_bytes=64)
+        nc.sync.dma_start(xw[:], x_words[0].rearrange("p n t -> p (n t)").bitcast(I32))
+        n2_t = load_list(n2, "n2_t")
+        sl_t = load_dealt(sl, "sl_t")
+        th_t = load_dealt(th, "th_t")
+        mem_rows = mem.rearrange("(p t) w -> t p w", t=PACK)
+        page = []
+        for t in range(PACK):
+            pg = keep.tile([P, U], F32, name="page", tag="page%d" % t, align_bytes=64)
+            nc.sync.dma_start(pg[:], mem_rows[t])
+            page.append(pg)
+        gn_t = load_dealt(gn, "gn_t")
+        w2_raw = keep.tile([P, PACK, N], F32, name="w2_raw")
+        nc.sync.dma_start(w2_raw[:], w2.rearrange("(p j) c -> p j c", j=PACK))
+        n3_t = load_list(n3, "n3_t")
+        n4_t = load_list(n4, "n4_t")
+        n5_t = load_list(n5, "n5_t")
+        sl2_t = load_plain(sl2, "sl2_t")
+        th2_t = load_plain(th2, "th2_t")
+
+        w1_bf = keep.tile([P, PACK * H], BF16, name="w1_bf", align_bytes=64)
+        w1_dst = w1_bf[:].rearrange("p (t m j) -> p m j t", t=PACK, j=PACK)
+        w1_src = w1_raw[:].rearrange("p j (m t) -> p m j t", t=PACK)
+        nc.vector.tensor_copy(w1_dst[:, :96], w1_src[:, :96])
+        nc.scalar.copy(w1_dst[:, 96:], w1_src[:, 96:])
+        xs_g = keep.tile([P, S], U8, name="xs_g", align_bytes=64)
+        nc.vector.tensor_copy(xs_g[:], xs[:].indirect(offs_t[:]))
+        w1_codes = keep.tile([P, H], U32, name="w1_codes", align_bytes=64)
+        w1_scales = keep.tile([P, H], U8, name="w1_scales", align_bytes=64)
+        nc.vector.quantize_mx(out=w1_codes[:].bitcast(FP8X4), scales=w1_scales[:], in_=w1_bf[:])
+        xw_g = keep.tile([P, S], U32, name="xw_g", align_bytes=64)
+        nc.vector.tensor_copy(xw_g[:], xw[:].bitcast(U32).indirect(offs_t[:]))
+
+        bias1 = keep.tile([P, PACK], F32, name="bias1")
+        nc.vector.scalar_tensor_tensor(bias1[:], sl_t[:], -1.0, th_t[:], ALU.mult, ALU.mult)
+        ys, y_banks, sgs, es, fs, nws = [], [], [], [], [], []
+        for pair in range(2):
+            y_ps = psum.tile([P, 2 * S], F32, name="y_ps", tag="bank%d" % (6 + pair))
+            sg = keep.tile([P, 2 * S], F32, name="sg%d" % pair)
+            for t in (2 * pair, 2 * pair + 1):
+                cols = slice(t * P, (t + 1) * P)
+                nc.tensor.matmul_mx(
+                    out=y_ps[:, (t % 2) * S : (t % 2 + 1) * S], lhsT=w1_codes[:, cols].bitcast(FP8X4), lhsT_scale=w1_scales[:, cols],
+                    rhs=xw_g[:].bitcast(FP8X4), rhs_scale=xs_g[:], start=True, stop=True,
+                )
+            for t in (2 * pair, 2 * pair + 1):
+                y = keep.tile([P, S], F32, name="y%d" % t)
+                nc.scalar.copy(y[:], y_ps[:, (t % 2) * S : (t % 2 + 1) * S])
+                ys.append(y)
+            for t in (2 * pair, 2 * pair + 1):
+                for u in range(2):
+                    lo = (t % 2) * S + u * P
+                    nc.scalar.activation(
+                        sg[:, lo : lo + P], ys[t][:].indirect(n2_t[:, u * 8 : (u + 1) * 8]), SIGMOID,
+                        bias=bias1[:, t : t + 1], scale=sl_t[:, t : t + 1],
+                    )
+            y_banks.append(y_ps)
+            sgs.append(sg)
+            es.append(keep.tile([P, 2 * S], F32, name="e%d" % pair))
+
+        def step_e(t):
+            nc.vector.tensor_tensor(es[t // 2][:, (t % 2) * S : (t % 2 + 1) * S], page[t][:].indirect(n1_t[:]), ys[t][:], ALU.subtract)
+
+        def step_f(pair):
+            f = keep.tile([P, 2 * S], F32, name="f%d" % pair)
+            nc.vector.scalar_tensor_tensor(f[:], sgs[pair][:], 1.0, es[pair][:], ALU.subtract, ALU.mult)
+            fs.append(f)
+
+        def step_nw(pair):
+            for t in (2 * pair, 2 * pair + 1):
+                nw = keep.tile([P, S], F32, name="nw", tag="nw%d" % t, align_bytes=64)
+                nc.vector.tensor_tensor(nw[:], ys[t][:], fs[pair][:, (t % 2) * S : (t % 2 + 1) * S], ALU.subtract)
+                nws.append(nw)
+
+        step_e(0)
+        step_e(1)
+        step_f(0)
+        step_e(2)
+        step_nw(0)
+        step_e(3)
+        step_f(1)
+        step_nw(1)
+        for t in range(PACK - 1):
+            nc.scalar.activation(page[t][:].indirect(n1_t[:]), nws[t][:], COPY)
+        nc.vector.tensor_copy(page[3][:].indirect(n1_t[:]), nws[3][:])
+
+        both = keep.tile([P, 2, PACK, HALF], BF16, name="planes", tag="nw3", align_bytes=64)
+        planes = [both[:, 0], both[:, 1]]
+        for t in (0, 3, 1, 2):
+            for c in range(2):
+                src = page[t][:, c * HALF : (c + 1) * HALF]
+                if t == 2:
+                    nc.scalar.activation(planes[c][:, t, :], src, COPY, scale=gn_t[:, t : t + 1])
+                else:
+                    nc.vector.tensor_scalar(planes[c][:, t, :], src, gn_t[:, t : t + 1], None, ALU.mult)
+
+        bias2 = keep.tile([P, PACK], F32, name="bias2", tag="page0", align_bytes=64)
+        nc.vector.scalar_tensor_tensor(bias2[:], sl2_t[:], -1.0, th2_t[:], ALU.mult, ALU.mult)
+
+        w2_codes = []
+        w2_scales = []
+
+        def prepare_w2(m):
+            w2_bf = keep.tile([P, P, PACK], BF16, name="w2_bf", tag="page2", align_bytes=64)
+            nc.scalar.copy(
+                w2_bf[:].rearrange("p (c i) j -> p c j i", i=4),
+                w2_raw[:, :, m * P : (m + 1) * P].rearrange("p j (c i) -> p c j i", i=4),
+            )
+            codes = keep.tile([P, P], U32, name="w2_codes", tag="page1" if m == 0 else "w2_codes%d" % m, align_bytes=64)
+            scales = keep.tile([P, P], U8, name="w2_scales%d" % m, align_bytes=64)
+            nc.vector.quantize_mx(out=codes[:].bitcast(FP8X4), scales=scales[:], in_=w2_bf[:].rearrange("p c j -> p (c j)"))
+            w2_codes.append(codes)
+            w2_scales.append(scales)
+
+        prepare_w2(0)
+        z_codes = []
+        z_scales = []
+        z_bfs = [keep.tile([P, HALF, PACK], BF16, name="z_bf%d" % c, align_bytes=64) for c in range(2)]
+
+        def weave(engine_copy, c, lo, hi):
+            engine_copy(
+                z_bfs[c][:, lo:hi, :].rearrange("p (c i) t -> p c t i", i=4),
+                planes[c][:, :, lo:hi].rearrange("p t (c i) -> p c t i", i=4),
+            )
+
+        def quantise_z(c):
+            codes = keep.tile([P, HALF], U32, name="z_codes%d" % c, align_bytes=64)
+            scales = keep.tile([P, HALF], U8, name="z_scales%d" % c, align_bytes=64)
+            nc.vector.quantize_mx(out=codes[:].bitcast(FP8X4), scales=scales[:], in_=z_bfs[c][:].rearrange("p c t -> p (c t)"))
+            z_codes.append(codes)
+            z_scales.append(scales)
+
+        weave(nc.vector.tensor_copy, 0, 0, HALF)
+        weave(nc.scalar.copy, 1, 0, 384)
+        weave(nc.vector.tensor_copy, 1, 384, HALF)
+        quantise_z(0)
+        quantise_z(1)
+        prepare_w2(1)
+
+        hs = [keep.tile([P, U], F32, name="h%d" % m) for m in range(PACK)]
+        owns = {}
+        sg2s = {}
+        parts_a = {}
+        parts_b = {}
+
+        def product(m, c):
+            cols = slice(c * HALF, (c + 1) * HALF)
+            h_ps = psum.tile([P, HALF], F32, name="h_ps", tag="bank%d" % (2 * m + c))
+            nc.tensor.matmul_mx(
+                out=h_ps[:], lhsT=w2_codes[m][:].bitcast(FP8X4), lhsT_scale=w2_scales[m][:],
+                rhs=z_codes[c][:].bitcast(FP8X4), rhs_scale=z_scales[c][:], start=True, stop=True,
+            )
+            if (m, c) == (0, 1):
+                nc.vector.tensor_copy(hs[m][:, cols], h_ps[:])
+            else:
+                nc.scalar.copy(hs[m][:, cols], h_ps[:])
+
+        def step_own(m, c):
+            own = keep.tile([P, HALF], F32, name="own%d%d" % (m, c))
+            nc.scalar.activation(own[:], hs[m][:, c * HALF : (c + 1) * HALF], SIGMOID, bias=bias2[:, m : m + 1], scale=sl2_t[:, m : m + 1])
+            owns[m, c] = own
+
+        def step_sg2(m, c):
+            sg2 = keep.tile([P, HALF], F32, name="sg2%d%d" % (m, c))
+            nc.scalar.activation(sg2[:], hs[m][:].indirect(n3_t[:, c * 32 : (c + 1) * 32]), SIGMOID, bias=bias2[:, m : m + 1], scale=sl2_t[:, m : m + 1])
+            sg2s[m, c] = sg2
+
+        def step_fetch(m, c):
+            got = keep.tile([P, HALF], F32, name="got%d%d" % (m, c))
+            nc.scalar.activation(got[:], hs[m][:].indirect(n4_t[:, c * 32 : (c + 1) * 32]), COPY)
+            fetched[m, c] = got
+
+        def step_a(m, c):
+            a = ring.tile([P, HALF], F32, name="a")
+            if (m, c) in fetched:
+                nc.vector.tensor_tensor(a[:], fetched[m, c][:], owns[m, c][:], ALU.mult)
+            else:
+                nc.vector.tensor_tensor(a[:], hs[m][:].indirect(n4_t[:, c * 32 : (c + 1) * 32]), owns[m, c][:], ALU.mult)
+            parts_a[m, c] = a
+
+        def step_b(m, c, lo, hi):
+            if lo == 0:
+                parts_b[m, c] = ring.tile([P, HALF], F32, name="b")
+            first = c * 32 + lo // 16
+            last = c * 32 + hi // 16
+            nc.vector.tensor_tensor(parts_b[m, c][:, lo:hi], hs[m][:].indirect(n5_t[:, first:last]), sg2s[m, c][:, lo:hi], ALU.mult)
+
+        def step_res(m, c, lo, hi):
+            res = keep.tile([P, hi - lo], F32, name="res%d%d%d" % (m, c, lo))
+            nc.vector.tensor_tensor(res[:], parts_a[m, c][:, lo:hi], parts_b[m, c][:, lo:hi], ALU.add)
+            nc.sync.dma_start(out[m * P : (m + 1) * P, c * HALF + lo : c * HALF + hi], res[:])
+
+        fetched = {}
+        pieces = [(m, c) for m in range(PACK) for c in range(2)]
+        for k, (m, c) in enumerate(pieces):
+            if c == 0:
+                product(m, 0)
+                step_own(m, 0)
+                product(m, 1)
+                step_sg2(m, 0)
+            else:
+                step_own(m, 1)
+                if m > 0:
+                    step_fetch(m, 1)
+                step_sg2(m, 1)
+            if c == 1 and m + 2 < PACK:
+                prepare_w2(m + 2)
+            step_a(m, c)
+            if k + 1 < len(pieces):
+                if k > 0:
+                    step_res(*pieces[k - 1], 0, HALF)
+                step_b(m, c, 0, HALF)
+        m, c = pieces[-1]
+        step_b(m, c, 0, HALF // 2)
+        step_res(m, 0, 0, HALF)
+        step_b(m, c, HALF // 2, HALF)
+        step_res(m, c, 0, HALF // 2)
+        step_res(m, c, HALF // 2, HALF)

@@ -48,6 +48,10 @@ def tile_picked_layepgemx_none_p_kernel(
                 nc.sync.dma_start(dst[:], src.rearrange("(t p) o -> p (t o)", t=PACK))
             return dst
 
+        warm_in = keep.tile([P, 1], F32, name="warm_in")
+        nc.gpsimd.memset(warm_in[:], 0.0)
+        warm_out = keep.tile([P, 1], F32, name="warm_out")
+        nc.scalar.activation(warm_out[:], warm_in[:], SIGMOID)
         xs = keep.tile([P, T], U8, name="xs", align_bytes=64)
         nc.vector.memset(xs[:].bitcast(I32), 0)
         w1_raw = keep.tile([P, PACK, H], F32, name="w1_raw")

@@ -95,19 +95,24 @@ def tile_picked_layepgemx_none_p_kernel(
 
         bias1 = keep.tile([P, PACK], F32, name="bias1")
         nc.vector.scalar_tensor_tensor(bias1[:], sl_t[:], -1.0, th_t[:], ALU.mult, ALU.mult)
-        ys, y_banks, sgs, es, fs, nws = [], [], [], [], [], []
+        ys, sgs, es, fs, nws = [], [], [], [], {}
+        y_banks = []
+        for t in range(PACK):
+            cols = slice(t * P, (t + 1) * P)
+            y_ps = psum.tile([P, HALF], F32, name="y_ps", tag="bank%d" % (4 + t))
+            nc.tensor.matmul_mx(
+                out=y_ps[:, :S], lhsT=w1_codes[:, cols].bitcast(FP8X4), lhsT_scale=w1_scales[:, cols],
+                rhs=xw_g[:].bitcast(FP8X4), rhs_scale=xs_g[:], start=True, stop=True,
+            )
+            y_banks.append(y_ps)
         for pair in range(2):
-            y_ps = psum.tile([P, 2 * S], F32, name="y_ps", tag="bank%d" % (6 + pair))
             sg = keep.tile([P, 2 * S], F32, name="sg%d" % pair)
             for t in (2 * pair, 2 * pair + 1):
-                cols = slice(t * P, (t + 1) * P)
-                nc.tensor.matmul_mx(
-                    out=y_ps[:, (t % 2) * S : (t % 2 + 1) * S], lhsT=w1_codes[:, cols].bitcast(FP8X4), lhsT_scale=w1_scales[:, cols],
-                    rhs=xw_g[:].bitcast(FP8X4), rhs_scale=xs_g[:], start=True, stop=True,
-                )
-            for t in (2 * pair, 2 * pair + 1):
                 y = keep.tile([P, S], F32, name="y%d" % t)
-                nc.scalar.copy(y[:], y_ps[:, (t % 2) * S : (t % 2 + 1) * S])
+                if t == 0:
+                    nc.vector.tensor_copy(y[:], y_banks[t][:, :S])
+                else:
+                    nc.scalar.copy(y[:], y_banks[t][:, :S])
                 ys.append(y)
             for t in (2 * pair, 2 * pair + 1):
                 for u in range(2):
@@ -116,7 +121,6 @@ def tile_picked_layepgemx_none_p_kernel(
                         sg[:, lo : lo + P], ys[t][:].indirect(n2_t[:, u * 8 : (u + 1) * 8]), SIGMOID,
                         bias=bias1[:, t : t + 1], scale=sl_t[:, t : t + 1],
                     )
-            y_banks.append(y_ps)
             sgs.append(sg)
             es.append(keep.tile([P, 2 * S], F32, name="e%d" % pair))
 
@@ -128,11 +132,10 @@ def tile_picked_layepgemx_none_p_kernel(
             nc.vector.scalar_tensor_tensor(f[:], sgs[pair][:], 1.0, es[pair][:], ALU.subtract, ALU.mult)
             fs.append(f)
 
-        def step_nw(pair):
-            for t in (2 * pair, 2 * pair + 1):
-                nw = keep.tile([P, S], F32, name="nw", tag="nw%d" % t, align_bytes=64)
-                nc.vector.tensor_tensor(nw[:], ys[t][:], fs[pair][:, (t % 2) * S : (t % 2 + 1) * S], ALU.subtract)
-                nws.append(nw)
+        def step_nw(t):
+            nw = keep.tile([P, S], F32, name="nw", tag="nw%d" % t, align_bytes=64)
+            nc.vector.tensor_tensor(nw[:], ys[t][:], fs[t // 2][:, (t % 2) * S : (t % 2 + 1) * S], ALU.subtract)
+            nws[t] = nw
 
         step_e(0)
         step_e(1)
@@ -140,21 +143,21 @@ def tile_picked_layepgemx_none_p_kernel(
         step_e(2)
         step_nw(0)
         step_e(3)
-        step_f(1)
         step_nw(1)
+        step_f(1)
+        step_nw(3)
+        step_nw(2)
         for t in range(PACK - 1):
             nc.scalar.activation(page[t][:].indirect(n1_t[:]), nws[t][:], COPY)
         nc.vector.tensor_copy(page[3][:].indirect(n1_t[:]), nws[3][:])
 
-        both = keep.tile([P, 2, PACK, HALF], BF16, name="planes", tag="nw3", align_bytes=64)
-        planes = [both[:, 0], both[:, 1]]
-        for t in (0, 3, 1, 2):
-            for c in range(2):
-                src = page[t][:, c * HALF : (c + 1) * HALF]
-                if t == 2:
-                    nc.scalar.activation(planes[c][:, t, :], src, COPY, scale=gn_t[:, t : t + 1])
-                else:
-                    nc.vector.tensor_scalar(planes[c][:, t, :], src, gn_t[:, t : t + 1], None, ALU.mult)
+        planes = keep.tile([P, 2, PACK, HALF], BF16, name="planes", tag="nw3", align_bytes=64)
+        for t in (0, 1, 3):
+            nc.vector.tensor_scalar(
+                planes[:, :, t, :], page[t][:].rearrange("p (c w) -> p c w", c=2), gn_t[:, t : t + 1], None, ALU.mult
+            )
+        for c in range(2):
+            nc.scalar.activation(planes[:, c, 2, :], page[2][:, c * HALF : (c + 1) * HALF], COPY, scale=gn_t[:, 2:3])
 
         bias2 = keep.tile([P, PACK], F32, name="bias2", tag="page0", align_bytes=64)
         nc.vector.scalar_tensor_tensor(bias2[:], sl2_t[:], -1.0, th2_t[:], ALU.mult, ALU.mult)
@@ -174,48 +177,48 @@ def tile_picked_layepgemx_none_p_kernel(
             w2_codes.append(codes)
             w2_scales.append(scales)
 
-        prepare_w2(0)
-        z_codes = []
-        z_scales = []
         z_bfs = [keep.tile([P, HALF, PACK], BF16, name="z_bf%d" % c, align_bytes=64) for c in range(2)]
+        z_codes = [keep.tile([P, HALF], U32, name="z_codes%d" % c, align_bytes=64) for c in range(2)]
+        z_scales = [keep.tile([P, HALF], U8, name="z_scales%d" % c, align_bytes=64) for c in range(2)]
 
         def weave(engine_copy, c, lo, hi):
             engine_copy(
                 z_bfs[c][:, lo:hi, :].rearrange("p (c i) t -> p c t i", i=4),
-                planes[c][:, :, lo:hi].rearrange("p t (c i) -> p c t i", i=4),
+                planes[:, c, :, lo:hi].rearrange("p t (c i) -> p c t i", i=4),
             )
 
-        def quantise_z(c):
-            codes = keep.tile([P, HALF], U32, name="z_codes%d" % c, align_bytes=64)
-            scales = keep.tile([P, HALF], U8, name="z_scales%d" % c, align_bytes=64)
-            nc.vector.quantize_mx(out=codes[:].bitcast(FP8X4), scales=scales[:], in_=z_bfs[c][:].rearrange("p c t -> p (c t)"))
-            z_codes.append(codes)
-            z_scales.append(scales)
+        def quantise_z(c, lo, hi):
+            nc.vector.quantize_mx(
+                out=z_codes[c][:, lo:hi].bitcast(FP8X4), scales=z_scales[c][:, lo:hi],
+                in_=z_bfs[c][:, lo:hi, :].rearrange("p c t -> p (c t)"),
+            )
 
         weave(nc.vector.tensor_copy, 0, 0, HALF)
-        weave(nc.scalar.copy, 1, 0, 384)
+        prepare_w2(0)
+        weave(nc.scalar.copy, 1, 0, 256)
+        weave(nc.scalar.copy, 1, 256, 384)
+        quantise_z(0, 0, HALF)
         weave(nc.vector.tensor_copy, 1, 384, HALF)
-        quantise_z(0)
-        quantise_z(1)
+        quantise_z(1, 0, 256)
+        quantise_z(1, 256, HALF)
         prepare_w2(1)
 
-        hs = [keep.tile([P, U], F32, name="h%d" % m) for m in range(PACK)]
+        hs = [keep.tile([P, U], F32, name="h", tag="h%d" % m) for m in range(PACK)]
         owns = {}
         sg2s = {}
         parts_a = {}
         parts_b = {}
+        fetched = {}
+        banks_used = []
 
-        def product(m, c):
-            cols = slice(c * HALF, (c + 1) * HALF)
-            h_ps = psum.tile([P, HALF], F32, name="h_ps", tag="bank%d" % (2 * m + c))
+        def product(m, c, lo, hi, engine_copy):
+            h_ps = psum.tile([P, HALF], F32, name="h_ps", tag="bank%d" % (len(banks_used) % 8))
+            banks_used.append(h_ps)
             nc.tensor.matmul_mx(
-                out=h_ps[:], lhsT=w2_codes[m][:].bitcast(FP8X4), lhsT_scale=w2_scales[m][:],
-                rhs=z_codes[c][:].bitcast(FP8X4), rhs_scale=z_scales[c][:], start=True, stop=True,
+                out=h_ps[:, : hi - lo], lhsT=w2_codes[m][:].bitcast(FP8X4), lhsT_scale=w2_scales[m][:],
+                rhs=z_codes[c][:, lo:hi].bitcast(FP8X4), rhs_scale=z_scales[c][:, lo:hi], start=True, stop=True,
             )
-            if (m, c) == (0, 1):
-                nc.vector.tensor_copy(hs[m][:, cols], h_ps[:])
-            else:
-                nc.scalar.copy(hs[m][:, cols], h_ps[:])
+            engine_copy(hs[m][:, c * HALF + lo : c * HALF + hi], h_ps[:, : hi - lo])
 
         def step_own(m, c):
             own = keep.tile([P, HALF], F32, name="own%d%d" % (m, c))
@@ -229,52 +232,61 @@ def tile_picked_layepgemx_none_p_kernel(
 
         def step_fetch(m, c):
             got = keep.tile([P, HALF], F32, name="got%d%d" % (m, c))
-            nc.scalar.activation(got[:], hs[m][:].indirect(n4_t[:, c * 32 : (c + 1) * 32]), COPY)
+            step = 256 if m + 1 == PACK else HALF
+            for lo in range(0, HALF, step):
+                first = c * 32 + lo // 16
+                nc.scalar.activation(got[:, lo : lo + step], hs[m][:].indirect(n4_t[:, first : first + step // 16]), COPY)
             fetched[m, c] = got
 
         def step_a(m, c):
-            a = ring.tile([P, HALF], F32, name="a")
+            a = keep.tile([P, HALF], F32, name="a%d%d" % (m, c))
             if (m, c) in fetched:
-                nc.vector.tensor_tensor(a[:], fetched[m, c][:], owns[m, c][:], ALU.mult)
+                step = 256 if m + 1 == PACK else HALF
+                for lo in range(0, HALF, step):
+                    nc.vector.tensor_tensor(a[:, lo : lo + step], fetched[m, c][:, lo : lo + step], owns[m, c][:, lo : lo + step], ALU.mult)
             else:
                 nc.vector.tensor_tensor(a[:], hs[m][:].indirect(n4_t[:, c * 32 : (c + 1) * 32]), owns[m, c][:], ALU.mult)
             parts_a[m, c] = a
 
-        def step_b(m, c, lo, hi):
-            if lo == 0:
-                parts_b[m, c] = ring.tile([P, HALF], F32, name="b")
-            first = c * 32 + lo // 16
-            last = c * 32 + hi // 16
-            nc.vector.tensor_tensor(parts_b[m, c][:, lo:hi], hs[m][:].indirect(n5_t[:, first:last]), sg2s[m, c][:, lo:hi], ALU.mult)
+        def step_b(m, c):
+            b = keep.tile([P, HALF], F32, name="b%d%d" % (m, c))
+            nc.vector.tensor_tensor(b[:], hs[m][:].indirect(n5_t[:, c * 32 : (c + 1) * 32]), sg2s[m, c][:], ALU.mult)
+            parts_b[m, c] = b
 
-        def step_res(m, c, lo, hi):
-            res = keep.tile([P, hi - lo], F32, name="res%d%d%d" % (m, c, lo))
+        def step_res(m, c, lo=0, hi=HALF):
+            res = keep.tile([P, hi - lo], F32, name="res", tag="h%d" % m if c == 0 and m + 1 < PACK else "res%d%d%d" % (m, c, lo))
             nc.vector.tensor_tensor(res[:], parts_a[m, c][:, lo:hi], parts_b[m, c][:, lo:hi], ALU.add)
             nc.sync.dma_start(out[m * P : (m + 1) * P, c * HALF + lo : c * HALF + hi], res[:])
 
-        fetched = {}
-        pieces = [(m, c) for m in range(PACK) for c in range(2)]
-        for k, (m, c) in enumerate(pieces):
-            if c == 0:
-                product(m, 0)
-                step_own(m, 0)
-                product(m, 1)
-                step_sg2(m, 0)
-            else:
+        for m in range(PACK):
+            product(m, 0, 0, HALF, nc.scalar.copy)
+            step_own(m, 0)
+            if m == 0:
+                product(m, 1, 0, 256, nc.scalar.copy)
+                product(m, 1, 256, HALF, nc.vector.tensor_copy)
                 step_own(m, 1)
-                if m > 0:
-                    step_fetch(m, 1)
+                step_sg2(m, 0)
                 step_sg2(m, 1)
-            if c == 1 and m + 2 < PACK:
+            else:
+                product(m, 1, 0, HALF, nc.scalar.copy)
+                step_sg2(m, 0)
+                step_sg2(m, 1)
+                step_own(m, 1)
+                step_fetch(m, 1)
+            if m + 2 < PACK:
                 prepare_w2(m + 2)
-            step_a(m, c)
-            if k + 1 < len(pieces):
-                if k > 0:
-                    step_res(*pieces[k - 1], 0, HALF)
-                step_b(m, c, 0, HALF)
-        m, c = pieces[-1]
-        step_b(m, c, 0, HALF // 2)
-        step_res(m, 0, 0, HALF)
-        step_b(m, c, HALF // 2, HALF)
-        step_res(m, c, 0, HALF // 2)
-        step_res(m, c, HALF // 2, HALF)
+            step_a(m, 0)
+            if m == 0:
+                step_a(m, 1)
+            step_b(m, 0)
+            step_b(m, 1)
+            if m + 1 == PACK:
+                step_res(m, 0)
+                step_a(m, 1)
+            else:
+                if m > 0:
+                    step_a(m, 1)
+                step_res(m, 0)
+                step_res(m, 1)
+        step_res(PACK - 1, 1, 0, 256)
+        step_res(PACK - 1, 1, 256, HALF)

@@ -152,12 +152,11 @@ def tile_picked_layepgemx_none_p_kernel(
         nc.vector.tensor_copy(page[3][:].indirect(n1_t[:]), nws[3][:])
 
         planes = keep.tile([P, 2, PACK, HALF], BF16, name="planes", tag="nw3", align_bytes=64)
-        for t in (0, 1, 3):
+        nc.scalar.activation(planes[:, :, 1, :], page[1][:].rearrange("p (c w) -> p c w", c=2), COPY, scale=gn_t[:, 1:2])
+        for t in (0, 3, 2):
             nc.vector.tensor_scalar(
                 planes[:, :, t, :], page[t][:].rearrange("p (c w) -> p c w", c=2), gn_t[:, t : t + 1], None, ALU.mult
             )
-        for c in range(2):
-            nc.scalar.activation(planes[:, c, 2, :], page[2][:, c * HALF : (c + 1) * HALF], COPY, scale=gn_t[:, 2:3])
 
         bias2 = keep.tile([P, PACK], F32, name="bias2", tag="page0", align_bytes=64)
         nc.vector.scalar_tensor_tensor(bias2[:], sl2_t[:], -1.0, th2_t[:], ALU.mult, ALU.mult)
@@ -165,19 +164,21 @@ def tile_picked_layepgemx_none_p_kernel(
         w2_codes = []
         w2_scales = []
 
-        def prepare_w2(m):
-            w2_bf = keep.tile([P, P, PACK], BF16, name="w2_bf", tag="page2", align_bytes=64)
-            nc.scalar.copy(
+        def prepare_w2(first, count, engine_copy, bf_tag, codes_tag):
+            width = count * P
+            w2_bf = keep.tile([P, width, PACK], BF16, name="w2_bf", tag=bf_tag, align_bytes=64)
+            engine_copy(
                 w2_bf[:].rearrange("p (c i) j -> p c j i", i=4),
-                w2_raw[:, :, m * P : (m + 1) * P].rearrange("p j (c i) -> p c j i", i=4),
+                w2_raw[:, :, first * P : first * P + width].rearrange("p j (c i) -> p c j i", i=4),
             )
-            codes = keep.tile([P, P], U32, name="w2_codes", tag="page1" if m == 0 else "w2_codes%d" % m, align_bytes=64)
-            scales = keep.tile([P, P], U8, name="w2_scales%d" % m, align_bytes=64)
+            codes = keep.tile([P, width], U32, name="w2_codes", tag=codes_tag, align_bytes=64)
+            scales = keep.tile([P, width], U8, name="w2_scales%d" % first, align_bytes=64)
             nc.vector.quantize_mx(out=codes[:].bitcast(FP8X4), scales=scales[:], in_=w2_bf[:].rearrange("p c j -> p (c j)"))
-            w2_codes.append(codes)
-            w2_scales.append(scales)
+            for m in range(count):
+                w2_codes.append(codes[:, m * P : (m + 1) * P])
+                w2_scales.append(scales[:, m * P : (m + 1) * P])
 
-        z_bfs = [keep.tile([P, HALF, PACK], BF16, name="z_bf%d" % c, align_bytes=64) for c in range(2)]
+        z_bfs = [keep.tile([P, HALF, PACK], BF16, name="z_bf", tag="z_bf%d" % c, align_bytes=64) for c in range(2)]
         z_codes = [keep.tile([P, HALF], U32, name="z_codes%d" % c, align_bytes=64) for c in range(2)]
         z_scales = [keep.tile([P, HALF], U8, name="z_scales%d" % c, align_bytes=64) for c in range(2)]
 
@@ -194,14 +195,15 @@ def tile_picked_layepgemx_none_p_kernel(
             )
 
         weave(nc.vector.tensor_copy, 0, 0, HALF)
-        prepare_w2(0)
+        prepare_w2(0, 1, nc.scalar.copy, "page1", "page2")
         weave(nc.scalar.copy, 1, 0, 256)
         weave(nc.scalar.copy, 1, 256, 384)
         quantise_z(0, 0, HALF)
         weave(nc.vector.tensor_copy, 1, 384, HALF)
         quantise_z(1, 0, 256)
         quantise_z(1, 256, HALF)
-        prepare_w2(1)
+        prepare_w2(1, 1, nc.scalar.copy, "page1", "w2_codes1")
+        prepare_w2(2, 2, nc.vector.tensor_copy, "z_bf1", "w2_codes2")
 
         hs = [keep.tile([P, U], F32, name="h", tag="h%d" % m) for m in range(PACK)]
         owns = {}
@@ -215,7 +217,7 @@ def tile_picked_layepgemx_none_p_kernel(
             h_ps = psum.tile([P, HALF], F32, name="h_ps", tag="bank%d" % (len(banks_used) % 8))
             banks_used.append(h_ps)
             nc.tensor.matmul_mx(
-                out=h_ps[:, : hi - lo], lhsT=w2_codes[m][:].bitcast(FP8X4), lhsT_scale=w2_scales[m][:],
+                out=h_ps[:, : hi - lo], lhsT=w2_codes[m].bitcast(FP8X4), lhsT_scale=w2_scales[m],
                 rhs=z_codes[c][:, lo:hi].bitcast(FP8X4), rhs_scale=z_scales[c][:, lo:hi], start=True, stop=True,
             )
             engine_copy(hs[m][:, c * HALF + lo : c * HALF + hi], h_ps[:, : hi - lo])
@@ -273,8 +275,6 @@ def tile_picked_layepgemx_none_p_kernel(
                 step_sg2(m, 1)
                 step_own(m, 1)
                 step_fetch(m, 1)
-            if m + 2 < PACK:
-                prepare_w2(m + 2)
             step_a(m, 0)
             if m == 0:
                 step_a(m, 1)

from contextlib import ExitStack

import concourse.mybir as mybir

K, T, S, N, H, U = 512, 2048, 256, 512, 512, 1024
FLOPS = 2 * K * H * S + 2 * H * N * U

F32 = mybir.dt.float32
BF16 = mybir.dt.bfloat16
I32 = mybir.dt.int32
U32 = mybir.dt.uint32
U16 = mybir.dt.uint16
U8 = mybir.dt.uint8
FP8X4 = mybir.dt.float8_e4m3fn_x4
ALU = mybir.AluOpType
COPY = mybir.ActivationFunctionType.Copy
SIGMOID = mybir.ActivationFunctionType.Sigmoid

P = 128
PACK = 4
HALF = 512
LIST_COLS = 16


def tile_picked_layepgemx_none_p_kernel(
    tc, x_words, x_scales, w1, mem, sl, th, gn, w2, sl2, th2, offs, n1, n2, n3, n4, n5, out
):
    nc = tc.nc
    with ExitStack() as ctx:
        lists = ctx.enter_context(tc.tile_pool(name="lists", bufs=1))
        keep = ctx.enter_context(tc.tile_pool(name="keep", bufs=1))
        ring = ctx.enter_context(tc.tile_pool(name="ring", bufs=3))
        psum = ctx.enter_context(tc.psum_pool(name="psum", bufs=1))

        def load_list(src, name):
            dst = lists.tile(list(src.shape), U16, name=name)
            nc.sync.dma_start(dst[:], src)
            return dst

        def load_dealt(src, name):
            dst = keep.tile([P, PACK], F32, name=name)
            nc.sync.dma_start(dst[:], src.rearrange("(p t) o -> p (t o)", t=PACK))
            return dst

        def load_plain(src, name):
            dst = keep.tile([P, PACK], F32, name=name)
            with nc.allow_non_contiguous_dma(reason="one value a partition"):
                nc.sync.dma_start(dst[:], src.rearrange("(t p) o -> p (t o)", t=PACK))
            return dst

        warm_in = keep.tile([P, 1], F32, name="warm_in")
        nc.gpsimd.memset(warm_in[:], 0.0)
        warm_out = keep.tile([P, 1], F32, name="warm_out")
        nc.scalar.activation(warm_out[:], warm_in[:], SIGMOID)
        xs = keep.tile([P, T], U8, name="xs", align_bytes=64)
        nc.vector.memset(xs[:].bitcast(I32), 0)
        w1_raw = keep.tile([P, PACK, H], F32, name="w1_raw")
        nc.sync.dma_start(w1_raw[:], w1.rearrange("(p j) c -> p j c", j=PACK))
        offs_t = load_list(offs, "offs_t")
        n1_t = load_list(n1, "n1_t")
        for q in range(4):
            nc.sync.dma_start(xs[32 * q : 32 * q + 4, :].bitcast(I32), x_scales[0, 4 * q : 4 * q + 4, :].bitcast(I32))
        xw = keep.tile([P, T], I32, name="xw", align_bytes=64)
        nc.sync.dma_start(xw[:], x_words[0].rearrange("p n t -> p (n t)").bitcast(I32))
        n2_t = load_list(n2, "n2_t")
        sl_t = load_dealt(sl, "sl_t")
        th_t = load_dealt(th, "th_t")
        mem_rows = mem.rearrange("(p t) w -> t p w", t=PACK)
        page = []
        for t in range(PACK):
            pg = keep.tile([P, U], F32, name="page", tag="page%d" % t, align_bytes=64)
            nc.sync.dma_start(pg[:], mem_rows[t])
            page.append(pg)
        gn_t = load_dealt(gn, "gn_t")
        w2_raw = keep.tile([P, PACK, N], F32, name="w2_raw")
        nc.sync.dma_start(w2_raw[:], w2.rearrange("(p j) c -> p j c", j=PACK))
        n3_t = load_list(n3, "n3_t")
        n4_t = load_list(n4, "n4_t")
        n5_t = load_list(n5, "n5_t")
        sl2_t = load_plain(sl2, "sl2_t")
        th2_t = load_plain(th2, "th2_t")

        w1_bf = keep.tile([P, PACK * H], BF16, name="w1_bf", align_bytes=64)
        w1_dst = w1_bf[:].rearrange("p (t m j) -> p m j t", t=PACK, j=PACK)
        w1_src = w1_raw[:].rearrange("p j (m t) -> p m j t", t=PACK)
        nc.vector.tensor_copy(w1_dst[:, :96], w1_src[:, :96])
        nc.scalar.copy(w1_dst[:, 96:], w1_src[:, 96:])
        xs_g = keep.tile([P, S], U8, name="xs_g", align_bytes=64)
        nc.vector.tensor_copy(xs_g[:], xs[:].indirect(offs_t[:]))
        w1_codes = keep.tile([P, H], U32, name="w1_codes", align_bytes=64)
        w1_scales = keep.tile([P, H], U8, name="w1_scales", align_bytes=64)
        nc.vector.quantize_mx(out=w1_codes[:].bitcast(FP8X4), scales=w1_scales[:], in_=w1_bf[:])
        xw_g = keep.tile([P, S], U32, name="xw_g", align_bytes=64)
        nc.vector.tensor_copy(xw_g[:], xw[:].bitcast(U32).indirect(offs_t[:]))

        bias1 = keep.tile([P, PACK], F32, name="bias1")
        nc.vector.scalar_tensor_tensor(bias1[:], sl_t[:], -1.0, th_t[:], ALU.mult, ALU.mult)
        ys, sgs, es, fs, nws = [], [], [], [], {}
        y_banks = []
        for t in range(PACK):
            cols = slice(t * P, (t + 1) * P)
            y_ps = psum.tile([P, HALF], F32, name="y_ps", tag="bank%d" % (4 + t))
            nc.tensor.matmul_mx(
                out=y_ps[:, :S], lhsT=w1_codes[:, cols].bitcast(FP8X4), lhsT_scale=w1_scales[:, cols],
                rhs=xw_g[:].bitcast(FP8X4), rhs_scale=xs_g[:], start=True, stop=True,
            )
            y_banks.append(y_ps)
        for pair in range(2):
            sg = keep.tile([P, 2 * S], F32, name="sg%d" % pair)
            for t in (2 * pair, 2 * pair + 1):
                y = keep.tile([P, S], F32, name="y%d" % t)
                if t == 0:
                    nc.vector.tensor_copy(y[:], y_banks[t][:, :S])
                else:
                    nc.scalar.copy(y[:], y_banks[t][:, :S])
                ys.append(y)
            for t in (2 * pair, 2 * pair + 1):
                for u in range(2):
                    lo = (t % 2) * S + u * P
                    nc.scalar.activation(
                        sg[:, lo : lo + P], ys[t][:].indirect(n2_t[:, u * 8 : (u + 1) * 8]), SIGMOID,
                        bias=bias1[:, t : t + 1], scale=sl_t[:, t : t + 1],
                    )
            sgs.append(sg)
            es.append(keep.tile([P, 2 * S], F32, name="e%d" % pair))

        def step_e(t):
            nc.vector.tensor_tensor(es[t // 2][:, (t % 2) * S : (t % 2 + 1) * S], page[t][:].indirect(n1_t[:]), ys[t][:], ALU.subtract)

        def step_f(pair):
            f = keep.tile([P, 2 * S], F32, name="f%d" % pair)
            nc.vector.scalar_tensor_tensor(f[:], sgs[pair][:], 1.0, es[pair][:], ALU.subtract, ALU.mult)
            fs.append(f)

        def step_nw(t):
            nw = keep.tile([P, S], F32, name="nw", tag="nw%d" % t, align_bytes=64)
            nc.vector.tensor_tensor(nw[:], ys[t][:], fs[t // 2][:, (t % 2) * S : (t % 2 + 1) * S], ALU.subtract)
            nws[t] = nw

        step_e(0)
        step_e(1)
        step_f(0)
        step_e(2)
        step_nw(0)
        step_e(3)
        step_nw(1)
        step_f(1)
        step_nw(3)
        step_nw(2)
        for t in range(PACK - 1):
            nc.scalar.activation(page[t][:].indirect(n1_t[:]), nws[t][:], COPY)
        nc.vector.tensor_copy(page[3][:].indirect(n1_t[:]), nws[3][:])

        planes = keep.tile([P, 2, PACK, HALF], BF16, name="planes", tag="nw3", align_bytes=64)
        nc.scalar.activation(planes[:, :, 1, :], page[1][:].rearrange("p (c w) -> p c w", c=2), COPY, scale=gn_t[:, 1:2])
        for t in (0, 3, 2):
            nc.vector.tensor_scalar(
                planes[:, :, t, :], page[t][:].rearrange("p (c w) -> p c w", c=2), gn_t[:, t : t + 1], None, ALU.mult
            )

        bias2 = keep.tile([P, PACK], F32, name="bias2", tag="page0", align_bytes=64)
        nc.vector.scalar_tensor_tensor(bias2[:], sl2_t[:], -1.0, th2_t[:], ALU.mult, ALU.mult)

        w2_codes = []
        w2_scales = []

        def prepare_w2(first, count, engine_copy, bf_tag, codes_tag):
            width = count * P
            w2_bf = keep.tile([P, width, PACK], BF16, name="w2_bf", tag=bf_tag, align_bytes=64)
            engine_copy(
                w2_bf[:].rearrange("p (c i) j -> p c j i", i=4),
                w2_raw[:, :, first * P : first * P + width].rearrange("p j (c i) -> p c j i", i=4),
            )
            codes = keep.tile([P, width], U32, name="w2_codes", tag=codes_tag, align_bytes=64)
            scales = keep.tile([P, width], U8, name="w2_scales%d" % first, align_bytes=64)
            nc.vector.quantize_mx(out=codes[:].bitcast(FP8X4), scales=scales[:], in_=w2_bf[:].rearrange("p c j -> p (c j)"))
            for m in range(count):
                w2_codes.append(codes[:, m * P : (m + 1) * P])
                w2_scales.append(scales[:, m * P : (m + 1) * P])

        z_bfs = [keep.tile([P, HALF, PACK], BF16, name="z_bf", tag="z_bf%d" % c, align_bytes=64) for c in range(2)]
        z_codes = [keep.tile([P, HALF], U32, name="z_codes%d" % c, align_bytes=64) for c in range(2)]
        z_scales = [keep.tile([P, HALF], U8, name="z_scales%d" % c, align_bytes=64) for c in range(2)]

        def weave(engine_copy, c, lo, hi):
            engine_copy(
                z_bfs[c][:, lo:hi, :].rearrange("p (c i) t -> p c t i", i=4),
                planes[:, c, :, lo:hi].rearrange("p t (c i) -> p c t i", i=4),
            )

        def quantise_z(c, lo, hi):
            nc.vector.quantize_mx(
                out=z_codes[c][:, lo:hi].bitcast(FP8X4), scales=z_scales[c][:, lo:hi],
                in_=z_bfs[c][:, lo:hi, :].rearrange("p c t -> p (c t)"),
            )

        weave(nc.vector.tensor_copy, 0, 0, HALF)
        prepare_w2(0, 1, nc.scalar.copy, "page1", "page2")
        weave(nc.scalar.copy, 1, 0, 256)
        weave(nc.scalar.copy, 1, 256, 384)
        quantise_z(0, 0, HALF)
        weave(nc.vector.tensor_copy, 1, 384, HALF)
        quantise_z(1, 0, 256)
        quantise_z(1, 256, HALF)
        prepare_w2(1, 1, nc.scalar.copy, "page1", "w2_codes1")
        prepare_w2(2, 2, nc.vector.tensor_copy, "z_bf1", "w2_codes2")

        hs = [keep.tile([P, U], F32, name="h", tag="h%d" % m) for m in range(PACK)]
        owns = {}
        sg2s = {}
        parts_a = {}
        parts_b = {}
        fetched = {}
        banks_used = []

        def product(m, c, lo, hi, engine_copy):
            h_ps = psum.tile([P, HALF], F32, name="h_ps", tag="bank%d" % (len(banks_used) % 8))
            banks_used.append(h_ps)
            nc.tensor.matmul_mx(
                out=h_ps[:, : hi - lo], lhsT=w2_codes[m].bitcast(FP8X4), lhsT_scale=w2_scales[m],
                rhs=z_codes[c][:, lo:hi].bitcast(FP8X4), rhs_scale=z_scales[c][:, lo:hi], start=True, stop=True,
            )
            engine_copy(hs[m][:, c * HALF + lo : c * HALF + hi], h_ps[:, : hi - lo])

        def step_own(m, c):
            own = keep.tile([P, HALF], F32, name="own%d%d" % (m, c))
            nc.scalar.activation(own[:], hs[m][:, c * HALF : (c + 1) * HALF], SIGMOID, bias=bias2[:, m : m + 1], scale=sl2_t[:, m : m + 1])
            owns[m, c] = own

        def step_sg2(m, c):
            sg2 = keep.tile([P, HALF], F32, name="sg2%d%d" % (m, c))
            nc.scalar.activation(sg2[:], hs[m][:].indirect(n3_t[:, c * 32 : (c + 1) * 32]), SIGMOID, bias=bias2[:, m : m + 1], scale=sl2_t[:, m : m + 1])
            sg2s[m, c] = sg2

        def step_fetch(m, c):
            got = keep.tile([P, HALF], F32, name="got%d%d" % (m, c))
            step = 256 if m + 1 == PACK else HALF
            for lo in range(0, HALF, step):
                first = c * 32 + lo // 16
                nc.scalar.activation(got[:, lo : lo + step], hs[m][:].indirect(n4_t[:, first : first + step // 16]), COPY)
            fetched[m, c] = got

        def step_a(m, c):
            a = keep.tile([P, HALF], F32, name="a%d%d" % (m, c))
            if (m, c) in fetched:
                step = 256 if m + 1 == PACK else HALF
                for lo in range(0, HALF, step):
                    nc.vector.tensor_tensor(a[:, lo : lo + step], fetched[m, c][:, lo : lo + step], owns[m, c][:, lo : lo + step], ALU.mult)
            else:
                nc.vector.tensor_tensor(a[:], hs[m][:].indirect(n4_t[:, c * 32 : (c + 1) * 32]), owns[m, c][:], ALU.mult)
            parts_a[m, c] = a

        def step_b(m, c):
            b = keep.tile([P, HALF], F32, name="b%d%d" % (m, c))
            nc.vector.tensor_tensor(b[:], hs[m][:].indirect(n5_t[:, c * 32 : (c + 1) * 32]), sg2s[m, c][:], ALU.mult)
            parts_b[m, c] = b

        def step_res(m, c, lo=0, hi=HALF):
            res = keep.tile([P, hi - lo], F32, name="res", tag="h%d" % m if c == 0 and m + 1 < PACK else "res%d%d%d" % (m, c, lo))
            nc.vector.tensor_tensor(res[:], parts_a[m, c][:, lo:hi], parts_b[m, c][:, lo:hi], ALU.add)
            nc.sync.dma_start(out[m * P : (m + 1) * P, c * HALF + lo : c * HALF + hi], res[:])

        for m in range(PACK):
            product(m, 0, 0, HALF, nc.scalar.copy)
            step_own(m, 0)
            if m == 0:
                product(m, 1, 0, 256, nc.scalar.copy)
                product(m, 1, 256, HALF, nc.vector.tensor_copy)
                step_own(m, 1)
                step_sg2(m, 0)
                step_sg2(m, 1)
            else:
                product(m, 1, 0, HALF, nc.scalar.copy)
                step_sg2(m, 0)
                step_sg2(m, 1)
                step_own(m, 1)
                step_fetch(m, 1)
            step_a(m, 0)
            if m == 0:
                step_a(m, 1)
            step_b(m, 0)
            step_b(m, 1)
            if m + 1 == PACK:
                step_res(m, 0)
                step_a(m, 1)
            else:
                if m > 0:
                    step_a(m, 1)
                step_res(m, 0)
                step_res(m, 1)
        step_res(PACK - 1, 1, 0, 256)
        step_res(PACK - 1, 1, 256, HALF)
